import numpy as np
import ml_dtypes


def mxq(x, axis, fmt="e4m3"):
    dtype, down = {"e4m3": (ml_dtypes.float8_e4m3fn, 7), "e5m2": (ml_dtypes.float8_e5m2, 14)}[fmt]
    v = np.moveaxis(np.asarray(x, np.float32).astype(ml_dtypes.bfloat16).astype(np.float64), axis, -1)
    blocks = v.reshape(v.shape[:-1] + (-1, 32))
    amax = np.abs(blocks).max(-1, keepdims=True)
    byte = np.maximum(np.where(amax > 0, np.frexp(amax)[1] - 1 + 127, 0) - down, 1)
    scale = np.exp2(byte - 127.0)
    codes = (blocks / scale).astype(np.float32).astype(dtype).astype(np.float64)
    return np.moveaxis((codes * scale).reshape(v.shape), -1, axis)


WIDE = False


def mx_kscale(k):
    if not WIDE:
        return np.ones(k)
    levels = np.array([10, -10, 5, -5, 0])
    if k % 512:
        return np.exp2(np.random.permutation(np.resize(levels, k // 32))).repeat(32)
    a = np.empty((k // 512, 16))
    for p in range(k // 512):
        a[p, :8] = np.random.permutation(np.resize(levels, 8))
        for g in range(8):
            far = levels[np.abs(levels - a[p, g]) >= 10]
            a[p, g + 8] = far[np.random.randint(len(far))]
    return np.exp2(a.ravel()).repeat(32)


def f64(x):
    return np.asarray(x).astype(np.float64)


def striped(idx):
    return np.tile(idx.reshape(-1, 16).T, (8, 1)).astype(np.uint16)


def unstriped(offs):
    return offs[:16].T.reshape(-1).astype(np.int64)


def striped8(idx):
    return np.concatenate([x.reshape(-1, 16).T for x in idx]).astype(np.uint16)


def runs(offs, k):
    lists = np.stack([offs[16 * r : 16 * r + 16].T.reshape(-1) for r in range(8)]).astype(np.int64)
    return lists[np.arange(k) % 512 // 64]


def pack_weight(w):
    k, n = w.shape
    w = f64(np.asarray(w, np.float32).astype(ml_dtypes.bfloat16)).reshape(k // 32, 32, n)
    amax = np.abs(w).max(1)
    byte = np.clip(np.where(amax > 0, np.frexp(amax)[1] - 1 + 127 - 7, 1), 1, 254)
    scaled = (w * np.exp2(127.0 - byte)[:, None, :]).reshape(k, n).astype(np.float32)
    words = np.ascontiguousarray(scaled.reshape(k // 512, 128, 4, n).transpose(0, 1, 3, 2)).astype(ml_dtypes.float8_e4m3fn).view(np.uint8)
    return words, np.ascontiguousarray(byte.astype(np.uint8).reshape(k // 512, 16, n))


def unpack_weight(words, scales):
    g, p, n, _ = words.shape
    vals = np.ascontiguousarray(words).view(ml_dtypes.float8_e4m3fn).astype(np.float64) * np.repeat(np.exp2(scales.astype(np.float64) - 127.0), 8, axis=1)[..., None]
    return vals.transpose(0, 1, 3, 2).reshape(g * 512, n)


def sigmoid(v):
    return 1.0 / (1.0 + np.exp(-np.maximum(v, -700.0)))

def planes(y):
    n, m = y.shape
    v = y.astype(np.float32).astype(ml_dtypes.bfloat16).astype(np.float64).reshape(n // 32, 32, m)
    top = np.abs(v).max(1)
    byte = np.clip(np.where(top > 0, np.frexp(top)[1] - 1 + 127 - 7, 1), 1, 254)
    codes = (v * np.exp2(127.0 - byte)[:, None, :]).reshape(n, m).astype(np.float32).astype(ml_dtypes.float8_e4m3fn).view(np.uint8)
    words = codes.reshape(n // 512, 128, 4, m).transpose(0, 1, 3, 2)
    return np.ascontiguousarray(words), np.ascontiguousarray(byte.astype(np.uint8).reshape(n // 512, 16, m))


K, T, S, N, G, H = 512, 2048, 512, 512, 2048, 512


def setup_inputs():
    n = np.random.standard_normal
    s = mx_kscale(K)[:, None]
    u = mx_kscale(S)
    packed_xT = pack_weight(n((K, T)) * s)
    packed_dT = pack_weight(n((K, G)) / s)
    packed_w1 = pack_weight(n((H, N)) / np.sqrt(2 * H) / u[:, None])
    packed_w2 = pack_weight(n((K, N)) / np.sqrt(2 * K) / s)
    return {
        "x_words": packed_xT[0],
        "x_scales": packed_xT[1],
        "d_words": packed_dT[0],
        "d_scales": packed_dT[1],
        "gn": (np.random.uniform(0.5, 1.5, (H, 1)) * u[:, None]).astype(np.float32),
        "w1_words": packed_w1[0],
        "w1_scales": packed_w1[1],
        "w2_words": packed_w2[0],
        "w2_scales": packed_w2[1],
        "offs": striped(np.random.permutation(T)[:S]),
        "k1": striped8(np.random.randint(0, G, (8, H))),
        "n1": striped(np.random.permutation(S)),
        "n2": striped(np.random.permutation(S)),
        "two": striped(np.random.permutation(T)[:S]),
        "n3": striped8(np.stack([np.random.permutation(S) for _ in range(8)])),
        "n4": striped8(np.stack([np.random.permutation(S) for _ in range(8)])),
    }


def reference(x_words, x_scales, d_words, d_scales, gn, w1_words, w1_scales, w2_words, w2_scales, offs, k1, n1, n2, two, n3, n4):
    d_k1 = unpack_weight(d_words, d_scales)[np.arange(K)[:, None], runs(k1, K)]
    xq = unpack_weight(x_words, x_scales)[:, unstriped(offs)]
    s = 0.0625 * (d_k1.T @ xq)
    z = f64(gn) * (s - (np.minimum(s[:, unstriped(n1)], s[:, unstriped(n2)])))
    x_two = unpack_weight(x_words, x_scales)[:, unstriped(two)]
    h = unpack_weight(w1_words, w1_scales).T @ mxq(z, 0, "e4m3") + unpack_weight(w2_words, w2_scales).T @ x_two
    st = h[np.arange(N)[:, None], runs(n3, N)] - h
    out_0 = h * (sigmoid(st[np.arange(N)[:, None], runs(n4, N)]))
    return (out_0,) + planes(out_0)

@@ -1,0 +1,236 @@
+from contextlib import ExitStack
+
+import concourse.mybir as mybir
+
+F32 = mybir.dt.float32
+BF16 = mybir.dt.bfloat16
+I32 = mybir.dt.int32
+U32 = mybir.dt.uint32
+U16 = mybir.dt.uint16
+U8 = mybir.dt.uint8
+FP8X4 = mybir.dt.float8_e4m3fn_x4
+ALU = mybir.AluOpType
+ACT = mybir.ActivationFunctionType
+
+P = 128
+PACK = 4
+S = 512
+T = 2048
+FLOPS = 3 * 2 * 512 * 512 * 512
+
+Z_CHUNKS = [(0, 256), (256, 384), (384, 512)]
+Y_CHUNKS = [(0, 256), (256, 384), (384, 512)]
+
+
+def tile_picked_kmixunderhopd_none_po_kernel(
+    tc, x_words, x_scales, d_words, d_scales, gn, w1_words, w1_scales, w2_words, w2_scales,
+    offs, k1, n1, n2, two, n3, n4, out_0, out_1, out_2,
+):
+    nc = tc.nc
+
+    def words_of(dram):
+        return dram[0].rearrange("p n r -> p (n r)").bitcast(I32)
+
+    def entries(offsets, a, b):
+        return offsets[:, a // 16 : b // 16]
+
+    with ExitStack() as ctx:
+        lists = ctx.enter_context(tc.tile_pool(name="lists", bufs=1))
+        keep = ctx.enter_context(tc.tile_pool(name="keep", bufs=1))
+        psum = ctx.enter_context(tc.psum_pool(name="psum", bufs=1))
+
+        def load_list(dram, name):
+            tile = lists.tile([P, S // 16], U16, name=name)
+            nc.sync.dma_start(tile[:], dram)
+            return tile
+
+        def sb(shape, dtype, name, tag=None):
+            return keep.tile(shape, dtype, name=name, tag=tag or name, align_bytes=64)
+
+        k1_sb = load_list(k1, "k1_sb")
+        d_sc_table = sb([P, T], U8, "d_sc_table")
+        nc.scalar.dma_start(
+            d_sc_table[:].bitcast(I32),
+            d_scales[0].bitcast(I32).unsqueeze(1).to_broadcast([16, 8, T // 4]),
+        )
+        d_table = sb([P, T], I32, "d_table", tag="big")
+        nc.sync.dma_start(d_table[:], words_of(d_words))
+        offs_sb = load_list(offs, "offs_sb")
+        two_sb = load_list(two, "two_sb")
+        n1_sb = load_list(n1, "n1_sb")
+        n2_sb = load_list(n2, "n2_sb")
+        x_table = sb([P, T], I32, "x_table")
+        nc.sync.dma_start(x_table[:], words_of(x_words))
+        x_sc_table = sb([P, T], U8, "x_sc_table")
+        nc.vector.memset(x_sc_table[:].bitcast(I32), 0)
+        for q in range(4):
+            nc.gpsimd.dma_start(
+                x_sc_table[32 * q : 32 * q + 4, :].bitcast(I32),
+                x_scales[0].bitcast(I32)[4 * q : 4 * q + 4, :],
+            )
+        n3_sb = load_list(n3, "n3_sb")
+        n4_sb = load_list(n4, "n4_sb")
+        gain = sb([P, PACK], F32, "gain")
+        nc.gpsimd.dma_start(gain[:], gn.rearrange("(p t) o -> p (t o)", t=PACK))
+
+        key_sc = sb([P, S], U8, "key_sc")
+        nc.vector.memset(key_sc[:].bitcast(I32), 0)
+        d_sc_picked = sb([P, S], U8, "d_sc_picked")
+        nc.vector.tensor_copy(d_sc_picked[:], d_sc_table[:].indirect(k1_sb[:]))
+        d_sc_dealt = sb([P, S], U8, "d_sc_dealt", tag="small")
+        nc.vector.tensor_copy(
+            d_sc_dealt[:].rearrange("p (t c i) -> p c t i", t=PACK, i=16),
+            d_sc_picked[:].rearrange("p (c i t) -> p c t i", t=PACK, i=16),
+        )
+        for r in range(4):
+            nc.scalar.dma_start(key_sc[r:P:32, :].bitcast(I32), d_sc_dealt[8 * r : P : 32, :].bitcast(I32))
+
+        d_picked = sb([P, S], U32, "d_picked")
+        nc.vector.tensor_copy(d_picked[:], d_table[:].bitcast(U32).indirect(k1_sb[:]))
+        keys = sb([P, S], U32, "keys")
+        nc.vector.tensor_copy(
+            keys[:].rearrange("p (t c i) -> p c t i", t=PACK, i=4),
+            d_picked[:].rearrange("p (c i t) -> p c t i", t=PACK, i=4),
+        )
+
+        tok_sc = sb([P, S], U8, "tok_sc")
+        nc.vector.tensor_copy(tok_sc[:], x_sc_table[:].indirect(offs_sb[:]))
+        tok = sb([P, S], U32, "tok")
+        nc.vector.tensor_copy(tok[:], x_table[:].bitcast(U32).indirect(offs_sb[:]))
+
+        nonneg = sb([P, PACK], F32, "nonneg")
+        nc.gpsimd.tensor_scalar(nonneg[:], gain[:], 0.0, 2.0, ALU.is_ge, ALU.mult)
+        size = sb([P, PACK], F32, "size")
+        nc.scalar.activation(size[:], gain[:], ACT.Abs, scale=0.0625)
+        sign_row = sb([P, 64, PACK], BF16, "sign_row")
+        nc.gpsimd.tensor_scalar(
+            sign_row[:], nonneg[:].unsqueeze(1).to_broadcast([P, 64, PACK]), 1.0, -1.0, ALU.mult, ALU.add
+        )
+
+        w_raw = sb([P, 2, S], I32, "w_raw", tag="big")
+        nc.sync.dma_start(w_raw[:, 0, :], words_of(w1_words))
+        nc.sync.dma_start(w_raw[:, 1, :], words_of(w2_words))
+        w_sc_raw = sb([P, S], U8, "w_sc_raw", tag="small")
+        nc.gpsimd.memset(w_sc_raw[:].bitcast(I32), 0)
+        for a, dram in enumerate((w1_scales, w2_scales)):
+            for q in range(4):
+                nc.sync.dma_start(
+                    w_sc_raw[32 * q + 4 * a : 32 * q + 4 * a + 4, :].bitcast(I32),
+                    dram[0].bitcast(I32)[4 * q : 4 * q + 4, :],
+                )
+        w = sb([P, 2, S], I32, "w")
+        for a in (1, 0):
+            nc.gpsimd.tensor_copy(
+                w[:, a, :].rearrange("p (t c i) -> p c t i", t=PACK, i=4),
+                w_raw[:, a, :].rearrange("p (c i t) -> p c t i", t=PACK, i=4),
+            )
+        w_sc = sb([P, S], U8, "w_sc")
+        nc.gpsimd.tensor_copy(
+            w_sc[:].rearrange("p (t c i) -> p c t i", t=PACK, i=16),
+            w_sc_raw[:].rearrange("p (c i t) -> p c t i", t=PACK, i=16),
+        )
+
+        score = sb([P, PACK, S], F32, "score")
+        for t in range(PACK):
+            cols = slice(P * t, P * (t + 1))
+            bank = psum.tile([P, S], F32, name="s_bank", tag="s%d" % t)
+            nc.tensor.matmul_mx(
+                bank[:], lhsT=keys[:, cols].bitcast(FP8X4), lhsT_scale=key_sc[:, cols],
+                rhs=tok[:].bitcast(FP8X4), rhs_scale=tok_sc[:], start=True, stop=True,
+            )
+            if t % 2 == 0:
+                nc.scalar.activation(score[:, t, :], bank[:], ACT.Copy, scale=size[:, t : t + 1])
+            else:
+                nc.vector.tensor_scalar(score[:, t, :], bank[:], size[:, t : t + 1], None, ALU.mult)
+
+        tok2 = sb([P, S], U32, "tok2")
+        nc.vector.tensor_copy(tok2[:], x_table[:].bitcast(U32).indirect(two_sb[:]))
+        tok2_sc = sb([P, S], U8, "tok2_sc", tag="x_table")
+        nc.vector.tensor_copy(tok2_sc[:], x_sc_table[:].indirect(two_sb[:]))
+
+        h_banks = [psum.tile([P, S], F32, name="h_bank", tag="h%d" % t) for t in range(PACK)]
+        for t in range(PACK):
+            cols = slice(P * t, P * (t + 1))
+            nc.tensor.matmul_mx(
+                h_banks[t][:], lhsT=w[:, 1, cols].bitcast(FP8X4), lhsT_scale=w_sc[4:P, cols],
+                rhs=tok2[:].bitcast(FP8X4), rhs_scale=tok2_sc[:], start=True, stop=False,
+            )
+
+        for a, b in Z_CHUNKS:
+            n = b - a
+            near1 = sb([P, PACK, n], F32, "near1_%d" % a)
+            near2 = sb([P, PACK, n], F32, "near2_%d" % a)
+            for t in range(PACK):
+                nc.scalar.activation(near1[:, t, :], score[:, t, :].indirect(entries(n1_sb, a, b)), ACT.Copy)
+                if a == 0 and t == 3:
+                    nc.vector.tensor_copy(near2[:, t, :], score[:, t, :].indirect(entries(n2_sb, a, b)))
+                else:
+                    nc.scalar.activation(near2[:, t, :], score[:, t, :].indirect(entries(n2_sb, a, b)), ACT.Copy)
+            least = sb([P, PACK, n], F32, "least_%d" % a)
+            nc.vector.tensor_tensor(least[:], near1[:], near2[:], ALU.min)
+            z_abs = sb([P, n, PACK], BF16, "z_abs_%d" % a)
+            nc.vector.tensor_tensor(
+                z_abs[:].rearrange("p (c i) t -> p c t i", i=4),
+                score[:, :, a:b].rearrange("p t (c i) -> p c t i", i=4),
+                least[:].rearrange("p t (c i) -> p c t i", i=4),
+                ALU.subtract,
+            )
+            z = sb([P, n // 64, 64 * PACK], BF16, "z_%d" % a)
+            nc.vector.tensor_tensor(
+                z[:],
+                z_abs[:].rearrange("p (g j) t -> p g (j t)", j=64),
+                sign_row[:].rearrange("p j t -> p (j t)").unsqueeze(1).to_broadcast([P, n // 64, 64 * PACK]),
+                ALU.mult,
+            )
+            z_words = sb([P, n], U32, "z_words_%d" % a)
+            z_sc = sb([P, n], U8, "z_sc_%d" % a)
+            nc.vector.quantize_mx(z_words[:].bitcast(FP8X4), z_sc[:], z[:].rearrange("p g e -> p (g e)"))
+            for t in range(PACK):
+                cols = slice(P * t, P * (t + 1))
+                nc.tensor.matmul_mx(
+                    h_banks[t][:, a:b], lhsT=w[:, 0, cols].bitcast(FP8X4), lhsT_scale=w_sc[:, cols],
+                    rhs=z_words[:].bitcast(FP8X4), rhs_scale=z_sc[:], start=False, stop=(b == S),
+                )
+
+        h_rows = [sb([P, S], F32, "h_%d" % t) for t in range(PACK)]
+        for t in range(PACK):
+            if t == 1:
+                nc.scalar.copy(h_rows[t][:], h_banks[t][:])
+            else:
+                nc.vector.tensor_copy(h_rows[t][:], h_banks[t][:])
+        steps = []
+        for t in range(PACK):
+            far = sb([P, S], F32, "far_%d" % t)
+            for a in (0, S // 2):
+                b = a + S // 2
+                nc.scalar.activation(far[:, a:b], h_rows[t][:].indirect(entries(n3_sb, a, b)), ACT.Copy)
+            step = sb([P, S], F32, "step_%d" % t)
+            nc.vector.tensor_tensor(step[:], far[:], h_banks[t][:], ALU.subtract)
+            steps.append(step)
+
+        out_rows = out_0.rearrange("(p t) j -> p t j", t=PACK)
+        out_words = out_1[0].rearrange("p j r -> p (j r)").bitcast(I32)
+        y_sc = sb([P, S], U8, "y_sc")
+        for a, b in Y_CHUNKS:
+            n = b - a
+            y = sb([P, PACK, n], F32, "y_%d" % a)
+            for t in range(PACK):
+                gate = sb([P, n], F32, "gate_%d_%d" % (a, t))
+                nc.scalar.activation(gate[:], steps[t][:].indirect(entries(n4_sb, a, b)), ACT.Sigmoid)
+                nc.vector.tensor_tensor(y[:, t, :], gate[:], h_banks[t][:, a:b], ALU.mult)
+            nc.sync.dma_start(out_rows[:, :, a:b], y[:])
+            y_round = sb([P, n, PACK], BF16, "y_round_%d" % a)
+            nc.vector.tensor_copy(
+                y_round[:].rearrange("p (c i) t -> p c t i", i=4),
+                y[:].rearrange("p t (c i) -> p c t i", i=4),
+            )
+            y_words = sb([P, n], U32, "y_words_%d" % a)
+            nc.vector.quantize_mx(
+                y_words[:].bitcast(FP8X4), y_sc[:, a:b], y_round[:].rearrange("p j t -> p (j t)")
+            )
+            nc.sync.dma_start(out_words[:, a:b], y_words[:].bitcast(I32))
+        for q in range(4):
+            queue = nc.scalar if q % 2 else nc.sync
+            queue.dma_start(
+                out_2[0].bitcast(I32)[4 * q : 4 * q + 4, :], y_sc[32 * q : 32 * q + 4, :].bitcast(I32)
+            )

@@ -47,61 +47,68 @@ def tile_picked_kmixunderhopd_none_po_kernel(
         def sb(shape, dtype, name, tag=None):
             return keep.tile(shape, dtype, name=name, tag=tag or name, align_bytes=64)
 
+        def load_scale_table(dram, name):
+            tile = sb([P, T], U8, name)
+            nc.scalar.dma_start(
+                tile[:].bitcast(I32), dram[0].bitcast(I32).unsqueeze(1).to_broadcast([16, 8, T // 4])
+            )
+            return tile
+
         k1_sb = load_list(k1, "k1_sb")
-        d_sc_table = sb([P, T], U8, "d_sc_table")
-        nc.scalar.dma_start(
-            d_sc_table[:].bitcast(I32),
-            d_scales[0].bitcast(I32).unsqueeze(1).to_broadcast([16, 8, T // 4]),
-        )
+        offs_sb = load_list(offs, "offs_sb")
+        d_sc_table = load_scale_table(d_scales, "d_sc_table")
         d_table = sb([P, T], I32, "d_table", tag="big")
         nc.sync.dma_start(d_table[:], words_of(d_words))
-        offs_sb = load_list(offs, "offs_sb")
+        x_sc_table = load_scale_table(x_scales, "x_sc_table")
         two_sb = load_list(two, "two_sb")
         n1_sb = load_list(n1, "n1_sb")
         n2_sb = load_list(n2, "n2_sb")
         x_table = sb([P, T], I32, "x_table")
         nc.sync.dma_start(x_table[:], words_of(x_words))
-        x_sc_table = sb([P, T], U8, "x_sc_table")
-        nc.vector.memset(x_sc_table[:].bitcast(I32), 0)
-        for q in range(4):
-            nc.gpsimd.dma_start(
-                x_sc_table[32 * q : 32 * q + 4, :].bitcast(I32),
-                x_scales[0].bitcast(I32)[4 * q : 4 * q + 4, :],
-            )
         n3_sb = load_list(n3, "n3_sb")
         n4_sb = load_list(n4, "n4_sb")
         gain = sb([P, PACK], F32, "gain")
         nc.gpsimd.dma_start(gain[:], gn.rearrange("(p t) o -> p (t o)", t=PACK))
 
-        key_sc = sb([P, S], U8, "key_sc")
-        nc.vector.memset(key_sc[:].bitcast(I32), 0)
-        d_sc_picked = sb([P, S], U8, "d_sc_picked")
-        nc.vector.tensor_copy(d_sc_picked[:], d_sc_table[:].indirect(k1_sb[:]))
-        d_sc_dealt = sb([P, S], U8, "d_sc_dealt", tag="small")
-        nc.vector.tensor_copy(
-            d_sc_dealt[:].rearrange("p (t c i) -> p c t i", t=PACK, i=16),
-            d_sc_picked[:].rearrange("p (c i t) -> p c t i", t=PACK, i=16),
-        )
-        for r in range(4):
-            nc.scalar.dma_start(key_sc[r:P:32, :].bitcast(I32), d_sc_dealt[8 * r : P : 32, :].bitcast(I32))
+        warm = sb([P, 2], F32, "warm")
+        nc.vector.memset(warm[:, 0:1], 0.0)
+        nc.scalar.activation(warm[:, 1:2], warm[:, 0:1], ACT.Sigmoid)
 
-        d_picked = sb([P, S], U32, "d_picked")
+        def place_rows(queue, placed, picked):
+            for r in range(4):
+                queue.dma_start(placed[r:P:32, :].bitcast(I32), picked[8 * r : P : 32, :].bitcast(I32))
+
+        first_sc = sb([P, 2 * S], U8, "first_sc")
+        nc.vector.memset(first_sc[:].bitcast(I32), 0)
+        tok2_sc = sb([P, S], U8, "tok2_sc")
+        nc.vector.memset(tok2_sc[:].bitcast(I32), 0)
+        first_picked = sb([P, 2 * S], U8, "first_picked")
+        nc.vector.tensor_copy(first_picked[:, 0:S], d_sc_table[:].indirect(k1_sb[:]))
+        nc.vector.tensor_copy(first_picked[:, S : 2 * S], x_sc_table[:].indirect(offs_sb[:]))
+        place_rows(nc.scalar, first_sc, first_picked)
+        tok_sc = first_sc[:, S : 2 * S]
+
+        d_picked = sb([P, S], U32, "d_picked", tag="small")
         nc.vector.tensor_copy(d_picked[:], d_table[:].bitcast(U32).indirect(k1_sb[:]))
         keys = sb([P, S], U32, "keys")
         nc.vector.tensor_copy(
             keys[:].rearrange("p (t c i) -> p c t i", t=PACK, i=4),
             d_picked[:].rearrange("p (c i t) -> p c t i", t=PACK, i=4),
         )
-
-        tok_sc = sb([P, S], U8, "tok_sc")
-        nc.vector.tensor_copy(tok_sc[:], x_sc_table[:].indirect(offs_sb[:]))
         tok = sb([P, S], U32, "tok")
         nc.vector.tensor_copy(tok[:], x_table[:].bitcast(U32).indirect(offs_sb[:]))
+        key_sc = sb([P, S], U8, "key_sc")
+        nc.vector.tensor_copy(
+            key_sc[:].rearrange("p (t c i) -> p c t i", t=PACK, i=16),
+            first_sc[:, 0:S].rearrange("p (c i t) -> p c t i", t=PACK, i=16),
+        )
 
         nonneg = sb([P, PACK], F32, "nonneg")
         nc.gpsimd.tensor_scalar(nonneg[:], gain[:], 0.0, 2.0, ALU.is_ge, ALU.mult)
+        sign = sb([P, PACK], F32, "sign")
+        nc.gpsimd.tensor_scalar(sign[:], nonneg[:], -1.0, 0.0625, ALU.add, ALU.mult)
         size = sb([P, PACK], F32, "size")
-        nc.scalar.activation(size[:], gain[:], ACT.Abs, scale=0.0625)
+        nc.gpsimd.tensor_tensor(size[:], gain[:], sign[:], ALU.mult)
         sign_row = sb([P, 64, PACK], BF16, "sign_row")
         nc.gpsimd.tensor_scalar(
             sign_row[:], nonneg[:].unsqueeze(1).to_broadcast([P, 64, PACK]), 1.0, -1.0, ALU.mult, ALU.add
@@ -136,17 +143,18 @@ def tile_picked_kmixunderhopd_none_po_kernel(
             bank = psum.tile([P, S], F32, name="s_bank", tag="s%d" % t)
             nc.tensor.matmul_mx(
                 bank[:], lhsT=keys[:, cols].bitcast(FP8X4), lhsT_scale=key_sc[:, cols],
-                rhs=tok[:].bitcast(FP8X4), rhs_scale=tok_sc[:], start=True, stop=True,
+                rhs=tok[:].bitcast(FP8X4), rhs_scale=tok_sc, start=True, stop=True,
             )
             if t % 2 == 0:
                 nc.scalar.activation(score[:, t, :], bank[:], ACT.Copy, scale=size[:, t : t + 1])
             else:
                 nc.vector.tensor_scalar(score[:, t, :], bank[:], size[:, t : t + 1], None, ALU.mult)
 
-        tok2 = sb([P, S], U32, "tok2")
+        tok2 = sb([P, S], U32, "tok2", tag="first_picked")
         nc.vector.tensor_copy(tok2[:], x_table[:].bitcast(U32).indirect(two_sb[:]))
-        tok2_sc = sb([P, S], U8, "tok2_sc", tag="x_table")
-        nc.vector.tensor_copy(tok2_sc[:], x_sc_table[:].indirect(two_sb[:]))
+        tok2_picked = sb([P, S], U8, "tok2_picked", tag="keys")
+        nc.vector.tensor_copy(tok2_picked[:], x_sc_table[:].indirect(two_sb[:]))
+        place_rows(nc.sync, tok2_sc, tok2_picked)
 
         h_banks = [psum.tile([P, S], F32, name="h_bank", tag="h%d" % t) for t in range(PACK)]
         for t in range(PACK):
@@ -156,18 +164,22 @@ def tile_picked_kmixunderhopd_none_po_kernel(
                 rhs=tok2[:].bitcast(FP8X4), rhs_scale=tok2_sc[:], start=True, stop=False,
             )
 
+        split = Z_CHUNKS[0][1]
+        near_first = sb([P, 2 * PACK * split], F32, "near_first")
+        near_rest = sb([P, 2 * PACK * (S - split)], F32, "near_rest", tag="size")
         for a, b in Z_CHUNKS:
             n = b - a
-            near1 = sb([P, PACK, n], F32, "near1_%d" % a)
-            near2 = sb([P, PACK, n], F32, "near2_%d" % a)
+            room = near_first if a == 0 else near_rest[:, 2 * PACK * (a - split) : 2 * PACK * (b - split)]
+            near1 = room[:, 0 : PACK * n].rearrange("p (t j) -> p t j", t=PACK)
+            near2 = room[:, PACK * n : 2 * PACK * n].rearrange("p (t j) -> p t j", t=PACK)
             for t in range(PACK):
                 nc.scalar.activation(near1[:, t, :], score[:, t, :].indirect(entries(n1_sb, a, b)), ACT.Copy)
-                if a == 0 and t == 3:
+                if a == 0:
                     nc.vector.tensor_copy(near2[:, t, :], score[:, t, :].indirect(entries(n2_sb, a, b)))
                 else:
                     nc.scalar.activation(near2[:, t, :], score[:, t, :].indirect(entries(n2_sb, a, b)), ACT.Copy)
-            least = sb([P, PACK, n], F32, "least_%d" % a)
-            nc.vector.tensor_tensor(least[:], near1[:], near2[:], ALU.min)
+            least = sb([P, PACK, n], F32, "least_%d" % a, tag="z_256" if b == S else "least")
+            nc.vector.tensor_tensor(least[:], near1, near2, ALU.min)
             z_abs = sb([P, n, PACK], BF16, "z_abs_%d" % a)
             nc.vector.tensor_tensor(
                 z_abs[:].rearrange("p (c i) t -> p c t i", i=4),
@@ -211,13 +223,17 @@ def tile_picked_kmixunderhopd_none_po_kernel(
         out_rows = out_0.rearrange("(p t) j -> p t j", t=PACK)
         out_words = out_1[0].rearrange("p j r -> p (j r)").bitcast(I32)
         y_sc = sb([P, S], U8, "y_sc")
+        split = Y_CHUNKS[0][1]
+        gate_first = sb([P, PACK * split], F32, "gate_first", tag="h_3")
+        gate_rest = sb([P, PACK * (S - split)], F32, "gate_rest", tag="far_3")
         for a, b in Y_CHUNKS:
             n = b - a
+            room = gate_first if a == 0 else gate_rest[:, PACK * (a - split) : PACK * (b - split)]
             y = sb([P, PACK, n], F32, "y_%d" % a)
             for t in range(PACK):
-                gate = sb([P, n], F32, "gate_%d_%d" % (a, t))
-                nc.scalar.activation(gate[:], steps[t][:].indirect(entries(n4_sb, a, b)), ACT.Sigmoid)
-                nc.vector.tensor_tensor(y[:, t, :], gate[:], h_banks[t][:, a:b], ALU.mult)
+                gate = room[:, t * n : (t + 1) * n]
+                nc.scalar.activation(gate, steps[t][:].indirect(entries(n4_sb, a, b)), ACT.Sigmoid)
+                nc.vector.tensor_tensor(y[:, t, :], gate, h_banks[t][:, a:b], ALU.mult)
             nc.sync.dma_start(out_rows[:, :, a:b], y[:])
             y_round = sb([P, n, PACK], BF16, "y_round_%d" % a)
             nc.vector.tensor_copy(

@@ -18,7 +18,7 @@ S = 512
 T = 2048
 FLOPS = 3 * 2 * 512 * 512 * 512
 
-Z_CHUNKS = [(0, 256), (256, 384), (384, 512)]
+Z_CHUNKS = [(0, 128), (128, 256), (256, 384), (384, 512)]
 Y_CHUNKS = [(0, 256), (256, 384), (384, 512)]
 
 
@@ -92,8 +92,8 @@ def tile_picked_kmixunderhopd_none_po_kernel(
         nc.vector.tensor_copy(d_picked[:], d_table[:].bitcast(U32).indirect(k1_sb[:]))
         keys = sb([P, S], U32, "keys")
         nc.vector.tensor_copy(
-            keys[:].rearrange("p (t c i) -> p c t i", t=PACK, i=4),
-            d_picked[:].rearrange("p (c i t) -> p c t i", t=PACK, i=4),
+            keys[:].rearrange("p (u e c i) -> p c u i e", u=2, e=2, i=4),
+            d_picked[:].rearrange("p (c i u e) -> p c u i e", u=2, e=2, i=4),
         )
         tok = sb([P, S], U32, "tok")
         nc.vector.tensor_copy(tok[:], x_table[:].bitcast(U32).indirect(offs_sb[:]))
@@ -125,18 +125,6 @@ def tile_picked_kmixunderhopd_none_po_kernel(
                     w_sc_raw[32 * q + 4 * a : 32 * q + 4 * a + 4, :].bitcast(I32),
                     dram[0].bitcast(I32)[4 * q : 4 * q + 4, :],
                 )
-        w = sb([P, 2, S], I32, "w")
-        for a in (1, 0):
-            nc.gpsimd.tensor_copy(
-                w[:, a, :].rearrange("p (t c i) -> p c t i", t=PACK, i=4),
-                w_raw[:, a, :].rearrange("p (c i t) -> p c t i", t=PACK, i=4),
-            )
-        w_sc = sb([P, S], U8, "w_sc")
-        nc.gpsimd.tensor_copy(
-            w_sc[:].rearrange("p (t c i) -> p c t i", t=PACK, i=16),
-            w_sc_raw[:].rearrange("p (c i t) -> p c t i", t=PACK, i=16),
-        )
-
         score = sb([P, PACK, S], F32, "score")
         for t in range(PACK):
             cols = slice(P * t, P * (t + 1))
@@ -145,24 +133,40 @@ def tile_picked_kmixunderhopd_none_po_kernel(
                 bank[:], lhsT=keys[:, cols].bitcast(FP8X4), lhsT_scale=key_sc[:, cols],
                 rhs=tok[:].bitcast(FP8X4), rhs_scale=tok_sc, start=True, stop=True,
             )
-            if t % 2 == 0:
-                nc.scalar.activation(score[:, t, :], bank[:], ACT.Copy, scale=size[:, t : t + 1])
-            else:
-                nc.vector.tensor_scalar(score[:, t, :], bank[:], size[:, t : t + 1], None, ALU.mult)
+            nc.scalar.activation(score[:, t, :], bank[:], ACT.Copy, scale=size[:, t : t + 1])
 
         tok2 = sb([P, S], U32, "tok2", tag="first_picked")
         nc.vector.tensor_copy(tok2[:], x_table[:].bitcast(U32).indirect(two_sb[:]))
-        tok2_picked = sb([P, S], U8, "tok2_picked", tag="keys")
+        tok2_picked = sb([P, S], U8, "tok2_picked", tag="x_table")
         nc.vector.tensor_copy(tok2_picked[:], x_sc_table[:].indirect(two_sb[:]))
         place_rows(nc.sync, tok2_sc, tok2_picked)
 
+        w = sb([P, 2, S], I32, "w", tag="x_sc_table")
+        for a in (1, 0):
+            nc.vector.tensor_copy(
+                w[:, a, :].rearrange("p (u e c i) -> p c u i e", u=2, e=2, i=4),
+                w_raw[:, a, :].rearrange("p (c i u e) -> p c u i e", u=2, e=2, i=4),
+            )
+        w_sc = sb([P, S], U8, "w_sc", tag="big")
+        nc.vector.tensor_copy(
+            w_sc[:].rearrange("p (t c i) -> p c t i", t=PACK, i=16),
+            w_sc_raw[:].rearrange("p (c i t) -> p c t i", t=PACK, i=16),
+        )
+
         h_banks = [psum.tile([P, S], F32, name="h_bank", tag="h%d" % t) for t in range(PACK)]
-        for t in range(PACK):
+        h_rows = [sb([P, S], F32, "h_%d" % t) for t in range(PACK)]
+        last = Z_CHUNKS[-1][0]
+
+        def project_tokens(t, a, b, start):
             cols = slice(P * t, P * (t + 1))
             nc.tensor.matmul_mx(
-                h_banks[t][:], lhsT=w[:, 1, cols].bitcast(FP8X4), lhsT_scale=w_sc[4:P, cols],
-                rhs=tok2[:].bitcast(FP8X4), rhs_scale=tok2_sc[:], start=True, stop=False,
+                h_banks[t][:, a:b], lhsT=w[:, 1, cols].bitcast(FP8X4), lhsT_scale=w_sc[4:P, cols],
+                rhs=tok2[:, a:b].bitcast(FP8X4), rhs_scale=tok2_sc[:, a:b], start=start, stop=False,
             )
+
+        for t in range(PACK):
+            project_tokens(t, 0, S // 2, True)
+            project_tokens(t, S // 2, last, False)
 
         split = Z_CHUNKS[0][1]
         near_first = sb([P, 2 * PACK * split], F32, "near_first")
@@ -174,17 +178,22 @@ def tile_picked_kmixunderhopd_none_po_kernel(
             near2 = room[:, PACK * n : 2 * PACK * n].rearrange("p (t j) -> p t j", t=PACK)
             for t in range(PACK):
                 nc.scalar.activation(near1[:, t, :], score[:, t, :].indirect(entries(n1_sb, a, b)), ACT.Copy)
-                if a == 0:
+                if a == 0 or (t == 3 and b < S):
                     nc.vector.tensor_copy(near2[:, t, :], score[:, t, :].indirect(entries(n2_sb, a, b)))
                 else:
                     nc.scalar.activation(near2[:, t, :], score[:, t, :].indirect(entries(n2_sb, a, b)), ACT.Copy)
-            least = sb([P, PACK, n], F32, "least_%d" % a, tag="z_256" if b == S else "least")
-            nc.vector.tensor_tensor(least[:], near1, near2, ALU.min)
+            if b == S:
+                for t in range(PACK):
+                    nc.scalar.copy(h_rows[t][:, 0:last], h_banks[t][:, 0:last])
+                    project_tokens(t, last, S, True)
+            least = sb([P, PACK, n], F32, "least_%d" % a, tag="z_256" if b == S else "small")
+            for planes in ((slice(0, 3), slice(3, 4)) if b == S else (slice(0, 4),)):
+                nc.vector.tensor_tensor(least[:, planes, :], near1[:, planes, :], near2[:, planes, :], ALU.min)
             z_abs = sb([P, n, PACK], BF16, "z_abs_%d" % a)
             nc.vector.tensor_tensor(
-                z_abs[:].rearrange("p (c i) t -> p c t i", i=4),
-                score[:, :, a:b].rearrange("p t (c i) -> p c t i", i=4),
-                least[:].rearrange("p t (c i) -> p c t i", i=4),
+                z_abs[:].rearrange("p (c i) t -> p c t i", i=2),
+                score[:, :, a:b].rearrange("p t (c i) -> p c t i", i=2),
+                least[:].rearrange("p t (c i) -> p c t i", i=2),
                 ALU.subtract,
             )
             z = sb([P, n // 64, 64 * PACK], BF16, "z_%d" % a)
@@ -201,44 +210,49 @@ def tile_picked_kmixunderhopd_none_po_kernel(
                 cols = slice(P * t, P * (t + 1))
                 nc.tensor.matmul_mx(
                     h_banks[t][:, a:b], lhsT=w[:, 0, cols].bitcast(FP8X4), lhsT_scale=w_sc[:, cols],
-                    rhs=z_words[:].bitcast(FP8X4), rhs_scale=z_sc[:], start=False, stop=(b == S),
+                    rhs=z_words[:].bitcast(FP8X4), rhs_scale=z_sc[:], start=False, stop=(b >= last),
                 )
 
-        h_rows = [sb([P, S], F32, "h_%d" % t) for t in range(PACK)]
         for t in range(PACK):
-            if t == 1:
-                nc.scalar.copy(h_rows[t][:], h_banks[t][:])
+            if t == 0:
+                nc.scalar.copy(h_rows[t][:, last:S], h_banks[t][:, last:S])
             else:
-                nc.vector.tensor_copy(h_rows[t][:], h_banks[t][:])
+                nc.vector.tensor_copy(h_rows[t][:, last:S], h_banks[t][:, last:S])
         steps = []
         for t in range(PACK):
             far = sb([P, S], F32, "far_%d" % t)
             for a in (0, S // 2):
                 b = a + S // 2
                 nc.scalar.activation(far[:, a:b], h_rows[t][:].indirect(entries(n3_sb, a, b)), ACT.Copy)
-            step = sb([P, S], F32, "step_%d" % t)
+            step = sb([P, S], F32, "step_%d" % t, tag="gate_row" if t == 3 else None)
             nc.vector.tensor_tensor(step[:], far[:], h_banks[t][:], ALU.subtract)
             steps.append(step)
+            if t == 0:
+                gate_row = sb([P, S], F32, "gate_row")
+                nc.scalar.activation(gate_row[:], step[:], ACT.Sigmoid)
 
         out_rows = out_0.rearrange("(p t) j -> p t j", t=PACK)
         out_words = out_1[0].rearrange("p j r -> p (j r)").bitcast(I32)
         y_sc = sb([P, S], U8, "y_sc")
         split = Y_CHUNKS[0][1]
-        gate_first = sb([P, PACK * split], F32, "gate_first", tag="h_3")
-        gate_rest = sb([P, PACK * (S - split)], F32, "gate_rest", tag="far_3")
+        gate_first = sb([P, 3 * split], F32, "gate_first", tag="h_3")
+        gate_rest = sb([P, 3 * (S - split)], F32, "gate_rest", tag="far_3")
         for a, b in Y_CHUNKS:
             n = b - a
-            room = gate_first if a == 0 else gate_rest[:, PACK * (a - split) : PACK * (b - split)]
+            room = gate_first if a == 0 else gate_rest[:, 3 * (a - split) : 3 * (b - split)]
             y = sb([P, PACK, n], F32, "y_%d" % a)
-            for t in range(PACK):
-                gate = room[:, t * n : (t + 1) * n]
+            nc.vector.tensor_tensor(
+                y[:, 0, :], gate_row[:].indirect(entries(n4_sb, a, b)), h_rows[0][:, a:b], ALU.mult
+            )
+            for t in range(1, PACK):
+                gate = room[:, (t - 1) * n : t * n]
                 nc.scalar.activation(gate, steps[t][:].indirect(entries(n4_sb, a, b)), ACT.Sigmoid)
                 nc.vector.tensor_tensor(y[:, t, :], gate, h_banks[t][:, a:b], ALU.mult)
             nc.sync.dma_start(out_rows[:, :, a:b], y[:])
             y_round = sb([P, n, PACK], BF16, "y_round_%d" % a)
             nc.vector.tensor_copy(
-                y_round[:].rearrange("p (c i) t -> p c t i", i=4),
-                y[:].rearrange("p t (c i) -> p c t i", i=4),
+                y_round[:].rearrange("p (c i) t -> p c t i", i=2),
+                y[:].rearrange("p t (c i) -> p c t i", i=2),
             )
             y_words = sb([P, n], U32, "y_words_%d" % a)
             nc.vector.quantize_mx(

from contextlib import ExitStack

import concourse.mybir as mybir

F32 = mybir.dt.float32
BF16 = mybir.dt.bfloat16
I32 = mybir.dt.int32
U32 = mybir.dt.uint32
U16 = mybir.dt.uint16
U8 = mybir.dt.uint8
FP8X4 = mybir.dt.float8_e4m3fn_x4
ALU = mybir.AluOpType
ACT = mybir.ActivationFunctionType

P = 128
PACK = 4
S = 512
T = 2048
FLOPS = 3 * 2 * 512 * 512 * 512

Z_CHUNKS = [(0, 128), (128, 256), (256, 384), (384, 512)]
Y_CHUNKS = [(0, 256), (256, 384), (384, 512)]


def tile_picked_kmixunderhopd_none_po_kernel(
    tc, x_words, x_scales, d_words, d_scales, gn, w1_words, w1_scales, w2_words, w2_scales,
    offs, k1, n1, n2, two, n3, n4, out_0, out_1, out_2,
):
    nc = tc.nc

    def words_of(dram):
        return dram[0].rearrange("p n r -> p (n r)").bitcast(I32)

    def entries(offsets, a, b):
        return offsets[:, a // 16 : b // 16]

    with ExitStack() as ctx:
        lists = ctx.enter_context(tc.tile_pool(name="lists", bufs=1))
        keep = ctx.enter_context(tc.tile_pool(name="keep", bufs=1))
        psum = ctx.enter_context(tc.psum_pool(name="psum", bufs=1))

        def load_list(dram, name):
            tile = lists.tile([P, S // 16], U16, name=name)
            nc.sync.dma_start(tile[:], dram)
            return tile

        def sb(shape, dtype, name, tag=None):
            return keep.tile(shape, dtype, name=name, tag=tag or name, align_bytes=64)

        def load_scale_table(dram, name):
            tile = sb([P, T], U8, name)
            nc.scalar.dma_start(
                tile[:].bitcast(I32), dram[0].bitcast(I32).unsqueeze(1).to_broadcast([16, 8, T // 4])
            )
            return tile

        k1_sb = load_list(k1, "k1_sb")
        offs_sb = load_list(offs, "offs_sb")
        d_sc_table = load_scale_table(d_scales, "d_sc_table")
        d_table = sb([P, T], I32, "d_table", tag="big")
        nc.sync.dma_start(d_table[:], words_of(d_words))
        x_sc_table = load_scale_table(x_scales, "x_sc_table")
        two_sb = load_list(two, "two_sb")
        n1_sb = load_list(n1, "n1_sb")
        n2_sb = load_list(n2, "n2_sb")
        x_table = sb([P, T], I32, "x_table")
        nc.sync.dma_start(x_table[:], words_of(x_words))
        n3_sb = load_list(n3, "n3_sb")
        n4_sb = load_list(n4, "n4_sb")
        gain = sb([P, PACK], F32, "gain")
        nc.gpsimd.dma_start(gain[:], gn.rearrange("(p t) o -> p (t o)", t=PACK))

        warm = sb([P, 2], F32, "warm")
        nc.vector.memset(warm[:, 0:1], 0.0)
        nc.scalar.activation(warm[:, 1:2], warm[:, 0:1], ACT.Sigmoid)

        def place_rows(queue, placed, picked):
            for r in range(4):
                queue.dma_start(placed[r:P:32, :].bitcast(I32), picked[8 * r : P : 32, :].bitcast(I32))

        first_sc = sb([P, 2 * S], U8, "first_sc")
        nc.vector.memset(first_sc[:].bitcast(I32), 0)
        tok2_sc = sb([P, S], U8, "tok2_sc")
        nc.vector.memset(tok2_sc[:].bitcast(I32), 0)
        first_picked = sb([P, 2 * S], U8, "first_picked")
        nc.vector.tensor_copy(first_picked[:, 0:S], d_sc_table[:].indirect(k1_sb[:]))
        nc.vector.tensor_copy(first_picked[:, S : 2 * S], x_sc_table[:].indirect(offs_sb[:]))
        place_rows(nc.scalar, first_sc, first_picked)
        tok_sc = first_sc[:, S : 2 * S]

        d_picked = sb([P, S], U32, "d_picked", tag="small")
        nc.vector.tensor_copy(d_picked[:], d_table[:].bitcast(U32).indirect(k1_sb[:]))
        keys = sb([P, S], U32, "keys")
        nc.vector.tensor_copy(
            keys[:].rearrange("p (u e c i) -> p c u i e", u=2, e=2, i=4),
            d_picked[:].rearrange("p (c i u e) -> p c u i e", u=2, e=2, i=4),
        )
        tok = sb([P, S], U32, "tok")
        nc.vector.tensor_copy(tok[:], x_table[:].bitcast(U32).indirect(offs_sb[:]))
        key_sc = sb([P, S], U8, "key_sc")
        nc.vector.tensor_copy(
            key_sc[:].rearrange("p (t c i) -> p c t i", t=PACK, i=16),
            first_sc[:, 0:S].rearrange("p (c i t) -> p c t i", t=PACK, i=16),
        )

        nonneg = sb([P, PACK], F32, "nonneg")
        nc.gpsimd.tensor_scalar(nonneg[:], gain[:], 0.0, 2.0, ALU.is_ge, ALU.mult)
        sign = sb([P, PACK], F32, "sign")
        nc.gpsimd.tensor_scalar(sign[:], nonneg[:], -1.0, 0.0625, ALU.add, ALU.mult)
        size = sb([P, PACK], F32, "size")
        nc.gpsimd.tensor_tensor(size[:], gain[:], sign[:], ALU.mult)
        sign_row = sb([P, 64, PACK], BF16, "sign_row")
        nc.gpsimd.tensor_scalar(
            sign_row[:], nonneg[:].unsqueeze(1).to_broadcast([P, 64, PACK]), 1.0, -1.0, ALU.mult, ALU.add
        )

        w_raw = sb([P, 2, S], I32, "w_raw", tag="big")
        nc.sync.dma_start(w_raw[:, 0, :], words_of(w1_words))
        nc.sync.dma_start(w_raw[:, 1, :], words_of(w2_words))
        w_sc_raw = sb([P, S], U8, "w_sc_raw", tag="small")
        nc.gpsimd.memset(w_sc_raw[:].bitcast(I32), 0)
        for a, dram in enumerate((w1_scales, w2_scales)):
            for q in range(4):
                nc.sync.dma_start(
                    w_sc_raw[32 * q + 4 * a : 32 * q + 4 * a + 4, :].bitcast(I32),
                    dram[0].bitcast(I32)[4 * q : 4 * q + 4, :],
                )
        score = sb([P, PACK, S], F32, "score")
        for t in range(PACK):
            cols = slice(P * t, P * (t + 1))
            bank = psum.tile([P, S], F32, name="s_bank", tag="s%d" % t)
            nc.tensor.matmul_mx(
                bank[:], lhsT=keys[:, cols].bitcast(FP8X4), lhsT_scale=key_sc[:, cols],
                rhs=tok[:].bitcast(FP8X4), rhs_scale=tok_sc, start=True, stop=True,
            )
            nc.scalar.activation(score[:, t, :], bank[:], ACT.Copy, scale=size[:, t : t + 1])

        tok2 = sb([P, S], U32, "tok2", tag="first_picked")
        nc.vector.tensor_copy(tok2[:], x_table[:].bitcast(U32).indirect(two_sb[:]))
        tok2_picked = sb([P, S], U8, "tok2_picked", tag="x_table")
        nc.vector.tensor_copy(tok2_picked[:], x_sc_table[:].indirect(two_sb[:]))
        place_rows(nc.sync, tok2_sc, tok2_picked)

        w = sb([P, 2, S], I32, "w", tag="x_sc_table")
        for a in (1, 0):
            nc.vector.tensor_copy(
                w[:, a, :].rearrange("p (u e c i) -> p c u i e", u=2, e=2, i=4),
                w_raw[:, a, :].rearrange("p (c i u e) -> p c u i e", u=2, e=2, i=4),
            )
        w_sc = sb([P, S], U8, "w_sc", tag="big")
        nc.vector.tensor_copy(
            w_sc[:].rearrange("p (t c i) -> p c t i", t=PACK, i=16),
            w_sc_raw[:].rearrange("p (c i t) -> p c t i", t=PACK, i=16),
        )

        h_banks = [psum.tile([P, S], F32, name="h_bank", tag="h%d" % t) for t in range(PACK)]
        h_rows = [sb([P, S], F32, "h_%d" % t) for t in range(PACK)]
        last = Z_CHUNKS[-1][0]

        def project_tokens(t, a, b, start):
            cols = slice(P * t, P * (t + 1))
            nc.tensor.matmul_mx(
                h_banks[t][:, a:b], lhsT=w[:, 1, cols].bitcast(FP8X4), lhsT_scale=w_sc[4:P, cols],
                rhs=tok2[:, a:b].bitcast(FP8X4), rhs_scale=tok2_sc[:, a:b], start=start, stop=False,
            )

        for t in range(PACK):
            project_tokens(t, 0, S // 2, True)
            project_tokens(t, S // 2, last, False)

        split = Z_CHUNKS[0][1]
        near_first = sb([P, 2 * PACK * split], F32, "near_first")
        near_rest = sb([P, 2 * PACK * (S - split)], F32, "near_rest", tag="size")
        for a, b in Z_CHUNKS:
            n = b - a
            room = near_first if a == 0 else near_rest[:, 2 * PACK * (a - split) : 2 * PACK * (b - split)]
            near1 = room[:, 0 : PACK * n].rearrange("p (t j) -> p t j", t=PACK)
            near2 = room[:, PACK * n : 2 * PACK * n].rearrange("p (t j) -> p t j", t=PACK)
            for t in range(PACK):
                nc.scalar.activation(near1[:, t, :], score[:, t, :].indirect(entries(n1_sb, a, b)), ACT.Copy)
                if a == 0 or (t == 3 and b < S):
                    nc.vector.tensor_copy(near2[:, t, :], score[:, t, :].indirect(entries(n2_sb, a, b)))
                else:
                    nc.scalar.activation(near2[:, t, :], score[:, t, :].indirect(entries(n2_sb, a, b)), ACT.Copy)
            if b == S:
                for t in range(PACK):
                    nc.scalar.copy(h_rows[t][:, 0:last], h_banks[t][:, 0:last])
                    project_tokens(t, last, S, True)
            least = sb([P, PACK, n], F32, "least_%d" % a, tag="z_256" if b == S else "small")
            for planes in ((slice(0, 3), slice(3, 4)) if b == S else (slice(0, 4),)):
                nc.vector.tensor_tensor(least[:, planes, :], near1[:, planes, :], near2[:, planes, :], ALU.min)
            z_abs = sb([P, n, PACK], BF16, "z_abs_%d" % a)
            nc.vector.tensor_tensor(
                z_abs[:].rearrange("p (c i) t -> p c t i", i=2),
                score[:, :, a:b].rearrange("p t (c i) -> p c t i", i=2),
                least[:].rearrange("p t (c i) -> p c t i", i=2),
                ALU.subtract,
            )
            z = sb([P, n // 64, 64 * PACK], BF16, "z_%d" % a)
            nc.vector.tensor_tensor(
                z[:],
                z_abs[:].rearrange("p (g j) t -> p g (j t)", j=64),
                sign_row[:].rearrange("p j t -> p (j t)").unsqueeze(1).to_broadcast([P, n // 64, 64 * PACK]),
                ALU.mult,
            )
            z_words = sb([P, n], U32, "z_words_%d" % a)
            z_sc = sb([P, n], U8, "z_sc_%d" % a)
            nc.vector.quantize_mx(z_words[:].bitcast(FP8X4), z_sc[:], z[:].rearrange("p g e -> p (g e)"))
            for t in range(PACK):
                cols = slice(P * t, P * (t + 1))
                nc.tensor.matmul_mx(
                    h_banks[t][:, a:b], lhsT=w[:, 0, cols].bitcast(FP8X4), lhsT_scale=w_sc[:, cols],
                    rhs=z_words[:].bitcast(FP8X4), rhs_scale=z_sc[:], start=False, stop=(b >= last),
                )

        for t in range(PACK):
            if t == 0:
                nc.scalar.copy(h_rows[t][:, last:S], h_banks[t][:, last:S])
            else:
                nc.vector.tensor_copy(h_rows[t][:, last:S], h_banks[t][:, last:S])
        steps = []
        for t in range(PACK):
            far = sb([P, S], F32, "far_%d" % t)
            for a in (0, S // 2):
                b = a + S // 2
                nc.scalar.activation(far[:, a:b], h_rows[t][:].indirect(entries(n3_sb, a, b)), ACT.Copy)
            step = sb([P, S], F32, "step_%d" % t, tag="gate_row" if t == 3 else None)
            nc.vector.tensor_tensor(step[:], far[:], h_banks[t][:], ALU.subtract)
            steps.append(step)
            if t == 0:
                gate_row = sb([P, S], F32, "gate_row")
                nc.scalar.activation(gate_row[:], step[:], ACT.Sigmoid)

        out_rows = out_0.rearrange("(p t) j -> p t j", t=PACK)
        out_words = out_1[0].rearrange("p j r -> p (j r)").bitcast(I32)
        y_sc = sb([P, S], U8, "y_sc")
        split = Y_CHUNKS[0][1]
        gate_first = sb([P, 3 * split], F32, "gate_first", tag="h_3")
        gate_rest = sb([P, 3 * (S - split)], F32, "gate_rest", tag="far_3")
        for a, b in Y_CHUNKS:
            n = b - a
            room = gate_first if a == 0 else gate_rest[:, 3 * (a - split) : 3 * (b - split)]
            y = sb([P, PACK, n], F32, "y_%d" % a)
            nc.vector.tensor_tensor(
                y[:, 0, :], gate_row[:].indirect(entries(n4_sb, a, b)), h_rows[0][:, a:b], ALU.mult
            )
            for t in range(1, PACK):
                gate = room[:, (t - 1) * n : t * n]
                nc.scalar.activation(gate, steps[t][:].indirect(entries(n4_sb, a, b)), ACT.Sigmoid)
                nc.vector.tensor_tensor(y[:, t, :], gate, h_banks[t][:, a:b], ALU.mult)
            nc.sync.dma_start(out_rows[:, :, a:b], y[:])
            y_round = sb([P, n, PACK], BF16, "y_round_%d" % a)
            nc.vector.tensor_copy(
                y_round[:].rearrange("p (c i) t -> p c t i", i=2),
                y[:].rearrange("p t (c i) -> p c t i", i=2),
            )
            y_words = sb([P, n], U32, "y_words_%d" % a)
            nc.vector.quantize_mx(
                y_words[:].bitcast(FP8X4), y_sc[:, a:b], y_round[:].rearrange("p j t -> p (j t)")
            )
            nc.sync.dma_start(out_words[:, a:b], y_words[:].bitcast(I32))
        for q in range(4):
            queue = nc.scalar if q % 2 else nc.sync
            queue.dma_start(
                out_2[0].bitcast(I32)[4 * q : 4 * q + 4, :], y_sc[32 * q : 32 * q + 4, :].bitcast(I32)
            )
